import numpy as np
import ml_dtypes


def mxq(x, axis, fmt="e4m3"):
    dtype, down = {"e4m3": (ml_dtypes.float8_e4m3fn, 7), "e5m2": (ml_dtypes.float8_e5m2, 14)}[fmt]
    v = np.moveaxis(np.asarray(x, np.float32).astype(ml_dtypes.bfloat16).astype(np.float64), axis, -1)
    blocks = v.reshape(v.shape[:-1] + (-1, 32))
    amax = np.abs(blocks).max(-1, keepdims=True)
    byte = np.maximum(np.where(amax > 0, np.frexp(amax)[1] - 1 + 127, 0) - down, 1)
    scale = np.exp2(byte - 127.0)
    codes = (blocks / scale).astype(np.float32).astype(dtype).astype(np.float64)
    return np.moveaxis((codes * scale).reshape(v.shape), -1, axis)


WIDE = False


def mx_kscale(k):
    if not WIDE:
        return np.ones(k)
    levels = np.array([10, -10, 5, -5, 0])
    if k % 512:
        return np.exp2(np.random.permutation(np.resize(levels, k // 32))).repeat(32)
    a = np.empty((k // 512, 16))
    for p in range(k // 512):
        a[p, :8] = np.random.permutation(np.resize(levels, 8))
        for g in range(8):
            far = levels[np.abs(levels - a[p, g]) >= 10]
            a[p, g + 8] = far[np.random.randint(len(far))]
    return np.exp2(a.ravel()).repeat(32)


def f64(x):
    return np.asarray(x).astype(np.float64)


def striped(idx):
    return np.tile(idx.reshape(-1, 16).T, (8, 1)).astype(np.uint16)


def unstriped(offs):
    return offs[:16].T.reshape(-1).astype(np.int64)


def striped8(idx):
    return np.concatenate([x.reshape(-1, 16).T for x in idx]).astype(np.uint16)


def runs(offs, k):
    lists = np.stack([offs[16 * r : 16 * r + 16].T.reshape(-1) for r in range(8)]).astype(np.int64)
    return lists[np.arange(k) % 512 // 64]


def pack_weight(w):
    k, n = w.shape
    w = f64(np.asarray(w, np.float32).astype(ml_dtypes.bfloat16)).reshape(k // 32, 32, n)
    amax = np.abs(w).max(1)
    byte = np.clip(np.where(amax > 0, np.frexp(amax)[1] - 1 + 127 - 7, 1), 1, 254)
    scaled = (w * np.exp2(127.0 - byte)[:, None, :]).reshape(k, n).astype(np.float32)
    words = np.ascontiguousarray(scaled.reshape(k // 512, 128, 4, n).transpose(0, 1, 3, 2)).astype(ml_dtypes.float8_e4m3fn).view(np.uint8)
    return words, np.ascontiguousarray(byte.astype(np.uint8).reshape(k // 512, 16, n))


def unpack_weight(words, scales):
    g, p, n, _ = words.shape
    vals = np.ascontiguousarray(words).view(ml_dtypes.float8_e4m3fn).astype(np.float64) * np.repeat(np.exp2(scales.astype(np.float64) - 127.0), 8, axis=1)[..., None]
    return vals.transpose(0, 1, 3, 2).reshape(g * 512, n)


def sigmoid(v):
    return 1.0 / (1.0 + np.exp(-np.maximum(v, -700.0)))

def planes(y):
    n, m = y.shape
    v = y.astype(np.float32).astype(ml_dtypes.bfloat16).astype(np.float64).reshape(n // 32, 32, m)
    top = np.abs(v).max(1)
    byte = np.clip(np.where(top > 0, np.frexp(top)[1] - 1 + 127 - 7, 1), 1, 254)
    codes = (v * np.exp2(127.0 - byte)[:, None, :]).reshape(n, m).astype(np.float32).astype(ml_dtypes.float8_e4m3fn).view(np.uint8)
    words = codes.reshape(n // 512, 128, 4, m).transpose(0, 1, 3, 2)
    return np.ascontiguousarray(words), np.ascontiguousarray(byte.astype(np.uint8).reshape(n // 512, 16, m))


K, T, S, N = 512, 2048, 512, 512


def setup_inputs():
    n = np.random.standard_normal
    s = mx_kscale(K)[:, None]
    packed_xT = pack_weight(n((K, T)) * s)
    return {
        "x_words": packed_xT[0],
        "x_scales": packed_xT[1],
        "w1": (n((K, N)) / np.sqrt(K) / s).astype(np.float32),
        "w2": (n((K, N)) / np.sqrt(K) / s).astype(np.float32),
        "w3": (n((K, N)) / np.sqrt(K) / s).astype(np.float32),
        "num": n((N, S)).astype(np.float32),
        "den": np.random.uniform(0.5, 2.0, (N, S)).astype(np.float32),
        "offs": striped(np.random.permutation(T)[:S]),
        "par": striped8(np.random.randint(0, S, (8, S))),
    }


def reference(x_words, x_scales, w1, w2, w3, num, den, offs, par):
    xq = unpack_weight(x_words, x_scales)[:, unstriped(offs)]
    q = sigmoid(mxq(f64(w3), 0, "e4m3").T @ xq)
    ek = np.exp(0.5 * ((mxq(f64(w1), 0, "e4m3").T @ xq)))
    val = mxq(f64(w2), 0, "e4m3").T @ xq
    out_0 = q * ((f64(num)[np.arange(N)[:, None], runs(par, N)] + ek * val) / (f64(den)[np.arange(N)[:, None], runs(par, N)] + ek))
    return (out_0,) + planes(out_0)

@@ -1,0 +1,190 @@
+from contextlib import ExitStack
+
+import concourse.mybir as mybir
+
+K, T, S, N = 512, 2048, 512, 512
+FLOPS = 3 * 2 * K * N * S
+
+F32 = mybir.dt.float32
+BF16 = mybir.dt.bfloat16
+I32 = mybir.dt.int32
+U32 = mybir.dt.uint32
+U16 = mybir.dt.uint16
+U8 = mybir.dt.uint8
+FP8X4 = mybir.dt.float8_e4m3fn_x4
+ACT = mybir.ActivationFunctionType
+ALU = mybir.AluOpType
+
+P = 128
+PACK = 4
+HALF = S // 2
+LIST_COLS = HALF // 16
+M_SPLIT = 80
+
+
+def tile_picked_wkv8_none_po_kernel(tc, x_words, x_scales, w1, w2, w3, num, den, offs, par, out_0, out_1, out_2):
+    nc = tc.nc
+    with ExitStack() as ctx:
+        lists = ctx.enter_context(tc.tile_pool(name="lists", bufs=1))
+        keep = ctx.enter_context(tc.tile_pool(name="keep", bufs=1))
+        psum = ctx.enter_context(tc.psum_pool(name="psum", bufs=1))
+
+        offs_sb = lists.tile([P, S // 16], U16, name="offs_sb")
+        par_sb = lists.tile([P, S // 16], U16, name="par_sb")
+        warm = keep.tile([P, 8], F32, name="warm")
+        warm_out = keep.tile([P, 8], F32, name="warm_out")
+        nc.vector.memset(warm[:], 0.0)
+        nc.scalar.activation(out=warm_out[:], in_=warm[:], func=ACT.Exp)
+
+        xw = keep.tile([P, T], I32, name="xw")
+        xs = keep.tile([P, T], U8, name="xs")
+        nc.gpsimd.memset(xs[:].bitcast(I32), 0)
+        nc.sync.dma_start(offs_sb[:], offs)
+        for quad in range(4):
+            nc.sync.dma_start(xs[32 * quad : 32 * quad + 4, :].bitcast(I32), x_scales[0, 4 * quad : 4 * quad + 4, :].bitcast(I32))
+        nc.sync.dma_start(xw[:], x_words[0].rearrange("p n r -> p (n r)").bitcast(I32))
+
+        def load_weight(w, name):
+            raw = keep.tile([P, PACK, N], F32, name=name + "_raw", tag=name + "_raw")
+            nc.sync.dma_start(raw[:], w.rearrange("(p j) n -> p j n", j=PACK))
+            return raw
+
+        def load_planes(table, name):
+            planes = []
+            for t in range(PACK):
+                plane = keep.tile([P, S], F32, name="%s%d" % (name, t))
+                nc.sync.dma_start(plane[:], table.rearrange("(p t) s -> p t s", t=PACK)[:, t, :])
+                planes.append(plane)
+            return planes
+
+        raw1 = load_weight(w1, "w1")
+        raw3 = load_weight(w3, "w3")
+        nc.sync.dma_start(par_sb[:], par)
+        den_sb = load_planes(den, "den")
+        raw2 = load_weight(w2, "w2")
+        num_sb = load_planes(num, "num")
+
+        xg_words = []
+        xg_scales = []
+        for h in range(2):
+            cut = offs_sb[:, h * LIST_COLS : (h + 1) * LIST_COLS]
+            words = keep.tile([P, HALF], U32, name="xgw%d" % h, align_bytes=64)
+            scales = keep.tile([P, HALF], U8, name="xgs%d" % h, align_bytes=64)
+            nc.vector.tensor_copy(words[:], xw[:].bitcast(U32).indirect(cut))
+            nc.vector.tensor_copy(scales[:], xs[:].indirect(cut))
+            xg_words.append(words)
+            xg_scales.append(scales)
+
+        def round_weight(raw, name, split):
+            dealt = keep.tile([P, PACK, P, PACK], BF16, name=name + "_bf", align_bytes=64)
+            src = raw[:].rearrange("p j (m t) -> p m j t", t=PACK)
+            dst = dealt[:].rearrange("p t m j -> p m j t")
+            if split > 0:
+                nc.vector.tensor_copy(dst[:, :split], src[:, :split])
+            if split < P:
+                nc.scalar.copy(dst[:, split:], src[:, split:])
+            return dealt
+
+        def quantize_weight(dealt, name):
+            made = []
+            for pair in range(2):
+                codes = keep.tile([P, 2 * P], U32, name="%s_codes%d" % (name, pair), align_bytes=64)
+                scales = keep.tile([P, 2 * P], U8, name="%s_scales%d" % (name, pair), align_bytes=64)
+                nc.vector.quantize_mx(out=codes[:].bitcast(FP8X4), scales=scales[:],
+                                      in_=dealt[:, 2 * pair : 2 * pair + 2].rearrange("p t m j -> p (t m j)"))
+                made.append((codes, scales))
+            return made
+
+        units = [(h, pair) for h in range(2) for pair in range(2)]
+
+        def product(weight, h, pair, tag, bufs):
+            codes, scales = weight[pair]
+            acc = psum.tile([P, 2, HALF], F32, name="acc_" + tag, tag=tag, bufs=bufs)
+            for i in range(2):
+                cols = slice(i * P, (i + 1) * P)
+                nc.tensor.matmul_mx(out=acc[:, i, :], lhsT=codes[:, cols].bitcast(FP8X4), lhsT_scale=scales[:, cols],
+                                    rhs=xg_words[h][:].bitcast(FP8X4), rhs_scale=xg_scales[h][:], start=True, stop=True)
+            return acc
+
+        def halves(name):
+            return [keep.tile([P, PACK, HALF], F32, name="%s%d" % (name, h)) for h in range(2)]
+
+        def two(tile, pair):
+            return tile[:, 2 * pair : 2 * pair + 2, :]
+
+        q1 = quantize_weight(round_weight(raw1, "w1", 84), "w1")
+        ek = halves("ek")
+        for h, pair in units:
+            nc.scalar.activation(out=two(ek[h], pair), in_=product(q1, h, pair, "key", 2)[:], func=ACT.Exp, scale=0.5)
+        q3 = quantize_weight(round_weight(raw3, "w3", P), "w3")
+        th = halves("th")
+        for h, pair in units:
+            nc.scalar.activation(out=two(th[h], pair), in_=product(q3, h, pair, "gate", 2)[:], func=ACT.Tanh, scale=0.5)
+
+        def gather_add(total, planes, addend, first, width):
+            cut = par_sb[:, first // 16 : (first + width) // 16]
+            for t in range(PACK):
+                nc.vector.tensor_tensor(total[:, t, :], planes[t][:].indirect(cut),
+                                        addend[:, t, first % HALF : first % HALF + width], ALU.add)
+
+        dsum = halves("dsum")
+        for h in range(2):
+            gather_add(dsum[h], den_sb, ek[h], h * HALF, HALF)
+        q2 = quantize_weight(round_weight(raw2, "w2", 0), "w2")
+
+        share = halves("share")
+        for h, pair in units:
+            nc.vector.tensor_tensor(two(share[h], pair), product(q2, h, pair, "val", 4)[:], two(ek[h], pair), ALU.mult)
+
+        late = keep.tile([P, 2, 2, PACK * HALF], F32, name="late", tag="w2_raw")
+        inv = halves("inv")
+        for h in range(2):
+            nc.scalar.activation(out=late[:, h, 0, :], in_=dsum[h][:].rearrange("p t s -> p (t s)"), func=ACT.Abs_reciprocal_sqrt)
+            nc.scalar.activation(out=inv[h][:].rearrange("p t s -> p (t s)"), in_=late[:, h, 0, :], func=ACT.Square)
+            nc.scalar.activation(out=late[:, h, 1, :], in_=dsum[h][:].rearrange("p t s -> p (t s)"), func=ACT.Sign)
+
+        gate = [keep.tile([P, PACK, HALF], F32, name="gate%d" % h, tag="gate%d" % h) for h in range(2)]
+        factor = halves("factor")
+
+        def make_factor(h):
+            nc.vector.scalar_tensor_tensor(gate[h][:].rearrange("p t s -> p (t s)"), th[h][:].rearrange("p t s -> p (t s)"), 1.0, late[:, h, 1, :], ALU.add, ALU.mult)
+            nc.vector.scalar_tensor_tensor(factor[h][:], gate[h][:], 0.5, inv[h][:], ALU.mult, ALU.mult)
+
+        out_rows = out_0.rearrange("(p t) s -> p t s", t=PACK)
+        out_words = out_1[0].rearrange("p n r -> p (n r)").bitcast(I32)
+        out_scales = out_2[0].bitcast(I32)
+        y_scales = keep.tile([P, S], U8, name="y_scales", align_bytes=64)
+
+        def fetch_num(first, width, tag):
+            nsum = keep.tile([P, PACK, width], F32, name="nsum%d" % first, tag=tag)
+            gather_add(nsum, num_sb, share[first // HALF], first, width)
+            return nsum
+
+        def make_y(nsum, first, width, copy):
+            y = keep.tile([P, PACK, width], F32, name="y%d" % first)
+            nc.vector.tensor_tensor(y[:], nsum[:], factor[first // HALF][:, :, first % HALF : first % HALF + width], ALU.mult)
+            nc.sync.dma_start(out_rows[:, :, first : first + width], y[:])
+            y_bf = keep.tile([P, width, PACK], BF16, name="ybf%d" % first, align_bytes=64)
+            copy(y_bf[:].rearrange("p (c i) t -> p c t i", i=4), y[:].rearrange("p t (c i) -> p c t i", i=4))
+            return y_bf
+
+        def make_planes(y_bf, first, width):
+            cols = slice(first, first + width)
+            y_codes = keep.tile([P, width], I32, name="ycodes%d" % first, align_bytes=64)
+            nc.vector.quantize_mx(out=y_codes[:].bitcast(FP8X4), scales=y_scales[:, cols], in_=y_bf[:].rearrange("p c t -> p (c t)"))
+            nc.sync.dma_start(out_words[:, cols], y_codes[:])
+
+        n0 = fetch_num(0, 256, "nsum")
+        make_factor(0)
+        b0 = make_y(n0, 0, 256, nc.scalar.copy)
+        n1 = fetch_num(256, 128, "gate0")
+        make_factor(1)
+        b1 = make_y(n1, 256, 128, nc.scalar.copy)
+        n2 = fetch_num(384, 128, "gate1")
+        make_planes(b0, 0, 256)
+        b2 = make_y(n2, 384, 128, nc.vector.tensor_copy)
+        make_planes(b1, 256, 128)
+        make_planes(b2, 384, 128)
+        for quad in range(4):
+            queue = nc.sync if quad % 2 == 0 else nc.scalar
+            queue.dma_start(out_scales[4 * quad : 4 * quad + 4, :], y_scales[32 * quad : 32 * quad + 4, :].bitcast(I32))

@@ -19,7 +19,7 @@ P = 128
 PACK = 4
 HALF = S // 2
 LIST_COLS = HALF // 16
-M_SPLIT = 80
+BLOCK = 128
 
 
 def tile_picked_wkv8_none_po_kernel(tc, x_words, x_scales, w1, w2, w3, num, den, offs, par, out_0, out_1, out_2):
@@ -39,133 +39,137 @@ def tile_picked_wkv8_none_po_kernel(tc, x_words, x_scales, w1, w2, w3, num, den,
         xw = keep.tile([P, T], I32, name="xw")
         xs = keep.tile([P, T], U8, name="xs")
         nc.gpsimd.memset(xs[:].bitcast(I32), 0)
-        nc.sync.dma_start(offs_sb[:], offs)
-        for quad in range(4):
-            nc.sync.dma_start(xs[32 * quad : 32 * quad + 4, :].bitcast(I32), x_scales[0, 4 * quad : 4 * quad + 4, :].bitcast(I32))
-        nc.sync.dma_start(xw[:], x_words[0].rearrange("p n r -> p (n r)").bitcast(I32))
 
         def load_weight(w, name):
             raw = keep.tile([P, PACK, N], F32, name=name + "_raw", tag=name + "_raw")
             nc.sync.dma_start(raw[:], w.rearrange("(p j) n -> p j n", j=PACK))
             return raw
 
-        def load_planes(table, name):
-            planes = []
-            for t in range(PACK):
-                plane = keep.tile([P, S], F32, name="%s%d" % (name, t))
-                nc.sync.dma_start(plane[:], table.rearrange("(p t) s -> p t s", t=PACK)[:, t, :])
-                planes.append(plane)
-            return planes
+        def load_plane(table, name, t):
+            plane = keep.tile([P, S], F32, name="%s%d" % (name, t))
+            nc.sync.dma_start(plane[:], table.rearrange("(p t) s -> p t s", t=PACK)[:, t, :])
+            return plane
 
-        raw1 = load_weight(w1, "w1")
-        raw3 = load_weight(w3, "w3")
+        den_sb = []
         nc.sync.dma_start(par_sb[:], par)
-        den_sb = load_planes(den, "den")
+        den_sb.append(load_plane(den, "den", 0))
+        den_sb.append(load_plane(den, "den", 1))
+        for quad in range(4):
+            nc.sync.dma_start(xs[32 * quad : 32 * quad + 4, :].bitcast(I32), x_scales[0, 4 * quad : 4 * quad + 4, :].bitcast(I32))
+        nc.sync.dma_start(xw[:], x_words[0].rearrange("p n r -> p (n r)").bitcast(I32))
+        nc.sync.dma_start(offs_sb[:], offs)
+        raw1 = load_weight(w1, "w1")
         raw2 = load_weight(w2, "w2")
-        num_sb = load_planes(num, "num")
+        den_sb.append(load_plane(den, "den", 2))
+        den_sb.append(load_plane(den, "den", 3))
+        raw3 = load_weight(w3, "w3")
+        num_sb = [load_plane(num, "num", t) for t in range(PACK)]
 
-        xg_words = []
-        xg_scales = []
-        for h in range(2):
-            cut = offs_sb[:, h * LIST_COLS : (h + 1) * LIST_COLS]
-            words = keep.tile([P, HALF], U32, name="xgw%d" % h, align_bytes=64)
-            scales = keep.tile([P, HALF], U8, name="xgs%d" % h, align_bytes=64)
-            nc.vector.tensor_copy(words[:], xw[:].bitcast(U32).indirect(cut))
-            nc.vector.tensor_copy(scales[:], xs[:].indirect(cut))
-            xg_words.append(words)
-            xg_scales.append(scales)
+        def halves(name, tag=None, align_bytes=None):
+            return keep.tile([P, 2, PACK, HALF], F32, name=name, tag=tag or name, align_bytes=align_bytes)
 
-        def round_weight(raw, name, split):
-            dealt = keep.tile([P, PACK, P, PACK], BF16, name=name + "_bf", align_bytes=64)
-            src = raw[:].rearrange("p j (m t) -> p m j t", t=PACK)
-            dst = dealt[:].rearrange("p t m j -> p m j t")
+        def block(tile, u):
+            return tile[:, u // 2, :, u % 2 * BLOCK : (u % 2 + 1) * BLOCK]
+
+        def picked(plane, h):
+            return plane[:].indirect(par_sb[:, h * LIST_COLS : (h + 1) * LIST_COLS])
+
+        def round_weight(raw, name, split, tag):
+            dealt = keep.tile([P, PACK, P, PACK], BF16, name=name + "_bf", tag=tag, align_bytes=64)
+            src = raw[:].rearrange("p j (m t) -> p m t j", t=PACK)
+            dst = dealt[:].rearrange("p t m j -> p m t j")
             if split > 0:
-                nc.vector.tensor_copy(dst[:, :split], src[:, :split])
+                nc.scalar.copy(dst[:, :split], src[:, :split])
             if split < P:
-                nc.scalar.copy(dst[:, split:], src[:, split:])
+                nc.vector.tensor_copy(dst[:, split:], src[:, split:])
             return dealt
 
         def quantize_weight(dealt, name):
-            made = []
-            for pair in range(2):
-                codes = keep.tile([P, 2 * P], U32, name="%s_codes%d" % (name, pair), align_bytes=64)
-                scales = keep.tile([P, 2 * P], U8, name="%s_scales%d" % (name, pair), align_bytes=64)
-                nc.vector.quantize_mx(out=codes[:].bitcast(FP8X4), scales=scales[:],
-                                      in_=dealt[:, 2 * pair : 2 * pair + 2].rearrange("p t m j -> p (t m j)"))
-                made.append((codes, scales))
+            codes = keep.tile([P, N], U32, name=name + "_codes", tag=name + "_codes", align_bytes=64)
+            scales = keep.tile([P, N], U8, name=name + "_scales", align_bytes=64)
+            nc.vector.quantize_mx(out=codes[:].bitcast(FP8X4), scales=scales[:], in_=dealt[:].rearrange("p t m j -> p (t m j)"))
+            return codes, scales
+
+        den_early = keep.tile([P, 2, S], F32, name="den_early")
+        for t in range(2):
+            for h in range(2):
+                nc.vector.tensor_copy(den_early[:, t, h * HALF : (h + 1) * HALF], picked(den_sb[t], h))
+
+        xg_words = keep.tile([P, S], U32, name="xg_words", align_bytes=64)
+        xg_scales = keep.tile([P, S], U8, name="xg_scales", align_bytes=64)
+        nc.vector.tensor_copy(xg_words[:], xw[:].bitcast(U32).indirect(offs_sb[:]))
+        nc.vector.tensor_copy(xg_scales[:], xs[:].indirect(offs_sb[:]))
+
+        def product(weight, t, bank):
+            codes, scales = weight
+            acc = psum.tile([P, S], F32, name="bank%d" % bank, tag="bank%d" % bank)
+            cols = slice(t * P, (t + 1) * P)
+            nc.tensor.matmul_mx(out=acc[:], lhsT=codes[:, cols].bitcast(FP8X4), lhsT_scale=scales[:, cols],
+                                rhs=xg_words[:].bitcast(FP8X4), rhs_scale=xg_scales[:], start=True, stop=True)
+            return acc[:].rearrange("p (h s) -> p h s", h=2)
+
+        def activate(weight, name, func, first_bank):
+            made = halves(name)
+            for t in range(PACK):
+                nc.scalar.activation(out=made[:, :, t, :], in_=product(weight, t, first_bank + t), func=func, scale=0.5)
             return made
 
-        units = [(h, pair) for h in range(2) for pair in range(2)]
-
-        def product(weight, h, pair, tag, bufs):
-            codes, scales = weight[pair]
-            acc = psum.tile([P, 2, HALF], F32, name="acc_" + tag, tag=tag, bufs=bufs)
-            for i in range(2):
-                cols = slice(i * P, (i + 1) * P)
-                nc.tensor.matmul_mx(out=acc[:, i, :], lhsT=codes[:, cols].bitcast(FP8X4), lhsT_scale=scales[:, cols],
-                                    rhs=xg_words[h][:].bitcast(FP8X4), rhs_scale=xg_scales[h][:], start=True, stop=True)
-            return acc
-
-        def halves(name):
-            return [keep.tile([P, PACK, HALF], F32, name="%s%d" % (name, h)) for h in range(2)]
-
-        def two(tile, pair):
-            return tile[:, 2 * pair : 2 * pair + 2, :]
-
-        q1 = quantize_weight(round_weight(raw1, "w1", 84), "w1")
-        ek = halves("ek")
-        for h, pair in units:
-            nc.scalar.activation(out=two(ek[h], pair), in_=product(q1, h, pair, "key", 2)[:], func=ACT.Exp, scale=0.5)
-        q3 = quantize_weight(round_weight(raw3, "w3", P), "w3")
-        th = halves("th")
-        for h, pair in units:
-            nc.scalar.activation(out=two(th[h], pair), in_=product(q3, h, pair, "gate", 2)[:], func=ACT.Tanh, scale=0.5)
-
-        def gather_add(total, planes, addend, first, width):
-            cut = par_sb[:, first // 16 : (first + width) // 16]
-            for t in range(PACK):
-                nc.vector.tensor_tensor(total[:, t, :], planes[t][:].indirect(cut),
-                                        addend[:, t, first % HALF : first % HALF + width], ALU.add)
+        q1 = quantize_weight(round_weight(raw1, "w1", 64, "w1_bf"), "w1")
+        ek = []
+        for t in range(PACK):
+            plane = keep.tile([P, 2, HALF], F32, name="ek%d" % t)
+            nc.scalar.activation(out=plane[:], in_=product(q1, t, t), func=ACT.Exp, scale=0.5)
+            ek.append(plane)
+        q2 = quantize_weight(round_weight(raw2, "w2", 36, "w2_bf"), "w2")
 
         dsum = halves("dsum")
+        for t in range(2):
+            nc.vector.tensor_tensor(dsum[:, :, t, :], den_early[:, t, :].rearrange("p (h s) -> p h s", h=2), ek[t][:], ALU.add)
+        for t in range(2, PACK):
+            for h in range(2):
+                nc.vector.tensor_tensor(dsum[:, h, t, :], picked(den_sb[t], h), ek[t][:, h, :], ALU.add)
+
+        q3 = quantize_weight(round_weight(raw3, "w3", P, "w1_codes"), "w3")
+        sign = halves("sign", "w3_raw")
         for h in range(2):
-            gather_add(dsum[h], den_sb, ek[h], h * HALF, HALF)
-        q2 = quantize_weight(round_weight(raw2, "w2", 0), "w2")
+            nc.scalar.activation(out=sign[:, h], in_=dsum[:, h], func=ACT.Sign)
+        th = activate(q3, "th", ACT.Tanh, 0)
 
-        share = halves("share")
-        for h, pair in units:
-            nc.vector.tensor_tensor(two(share[h], pair), product(q2, h, pair, "val", 4)[:], two(ek[h], pair), ALU.mult)
+        share = halves("share", "w1_codes", 64)
+        for t in range(PACK):
+            nc.vector.tensor_tensor(share[:, :, t, :], product(q2, t, PACK + t), ek[t][:], ALU.mult)
+        nsum = halves("nsum")
+        for h in range(2):
+            for t in range(PACK):
+                nc.vector.tensor_tensor(nsum[:, h, t, :], picked(num_sb[t], h), share[:, h, t, :], ALU.add)
 
-        late = keep.tile([P, 2, 2, PACK * HALF], F32, name="late", tag="w2_raw")
         inv = halves("inv")
         for h in range(2):
-            nc.scalar.activation(out=late[:, h, 0, :], in_=dsum[h][:].rearrange("p t s -> p (t s)"), func=ACT.Abs_reciprocal_sqrt)
-            nc.scalar.activation(out=inv[h][:].rearrange("p t s -> p (t s)"), in_=late[:, h, 0, :], func=ACT.Square)
-            nc.scalar.activation(out=late[:, h, 1, :], in_=dsum[h][:].rearrange("p t s -> p (t s)"), func=ACT.Sign)
-
-        gate = [keep.tile([P, PACK, HALF], F32, name="gate%d" % h, tag="gate%d" % h) for h in range(2)]
-        factor = halves("factor")
-
-        def make_factor(h):
-            nc.vector.scalar_tensor_tensor(gate[h][:].rearrange("p t s -> p (t s)"), th[h][:].rearrange("p t s -> p (t s)"), 1.0, late[:, h, 1, :], ALU.add, ALU.mult)
-            nc.vector.scalar_tensor_tensor(factor[h][:], gate[h][:], 0.5, inv[h][:], ALU.mult, ALU.mult)
+            root = keep.tile([P, PACK, HALF], F32, name="root", tag="w3_codes", align_bytes=64)
+            nc.scalar.activation(out=root[:], in_=dsum[:, h], func=ACT.Abs_reciprocal_sqrt)
+            nc.scalar.activation(out=inv[:, h], in_=root[:], func=ACT.Square)
 
         out_rows = out_0.rearrange("(p t) s -> p t s", t=PACK)
         out_words = out_1[0].rearrange("p n r -> p (n r)").bitcast(I32)
         out_scales = out_2[0].bitcast(I32)
         y_scales = keep.tile([P, S], U8, name="y_scales", align_bytes=64)
+        y = halves("y")
 
-        def fetch_num(first, width, tag):
-            nsum = keep.tile([P, PACK, width], F32, name="nsum%d" % first, tag=tag)
-            gather_add(nsum, num_sb, share[first // HALF], first, width)
-            return nsum
+        def make_y(h, factor_tag):
+            factor = keep.tile([P, 2, PACK, BLOCK], F32, name="factor", tag=factor_tag, align_bytes=64)
+            gate = keep.tile([P, 2, PACK, BLOCK], F32, name="gate", tag="gate")
+            for b in range(2):
+                nc.vector.scalar_tensor_tensor(gate[:, b], block(th, 2 * h + b), 1.0, block(sign, 2 * h + b), ALU.add, ALU.mult)
+            for b in range(2):
+                nc.vector.scalar_tensor_tensor(factor[:, b], gate[:, b], 0.5, block(inv, 2 * h + b), ALU.mult, ALU.mult)
+            for b in range(2):
+                nc.vector.tensor_tensor(block(y, 2 * h + b), block(nsum, 2 * h + b), factor[:, b], ALU.mult)
 
-        def make_y(nsum, first, width, copy):
-            y = keep.tile([P, PACK, width], F32, name="y%d" % first)
-            nc.vector.tensor_tensor(y[:], nsum[:], factor[first // HALF][:, :, first % HALF : first % HALF + width], ALU.mult)
-            nc.sync.dma_start(out_rows[:, :, first : first + width], y[:])
-            y_bf = keep.tile([P, width, PACK], BF16, name="ybf%d" % first, align_bytes=64)
-            copy(y_bf[:].rearrange("p (c i) t -> p c t i", i=4), y[:].rearrange("p t (c i) -> p c t i", i=4))
+        def hand_out(first, width, copy):
+            part = y[:, first // HALF, :, first % HALF : first % HALF + width]
+            nc.sync.dma_start(out_rows[:, :, first : first + width], part)
+            y_bf = keep.tile([P, width, PACK], BF16, name="ybf%d" % first, tag="ybf%d" % first, align_bytes=64)
+            copy(y_bf[:].rearrange("p (c i) t -> p c t i", i=4), part.rearrange("p t (c i) -> p c t i", i=4))
             return y_bf
 
         def make_planes(y_bf, first, width):
@@ -174,17 +178,14 @@ def tile_picked_wkv8_none_po_kernel(tc, x_words, x_scales, w1, w2, w3, num, den,
             nc.vector.quantize_mx(out=y_codes[:].bitcast(FP8X4), scales=y_scales[:, cols], in_=y_bf[:].rearrange("p c t -> p (c t)"))
             nc.sync.dma_start(out_words[:, cols], y_codes[:])
 
-        n0 = fetch_num(0, 256, "nsum")
-        make_factor(0)
-        b0 = make_y(n0, 0, 256, nc.scalar.copy)
-        n1 = fetch_num(256, 128, "gate0")
-        make_factor(1)
-        b1 = make_y(n1, 256, 128, nc.scalar.copy)
-        n2 = fetch_num(384, 128, "gate1")
-        make_planes(b0, 0, 256)
-        b2 = make_y(n2, 384, 128, nc.vector.tensor_copy)
-        make_planes(b1, 256, 128)
-        make_planes(b2, 384, 128)
+        make_y(0, "factor")
+        b0 = hand_out(0, HALF, nc.scalar.copy)
+        make_planes(b0, 0, HALF)
+        make_y(1, "factor1")
+        b1 = hand_out(HALF, BLOCK, nc.scalar.copy)
+        b2 = hand_out(HALF + BLOCK, BLOCK, nc.vector.tensor_copy)
+        make_planes(b1, HALF, BLOCK)
+        make_planes(b2, HALF + BLOCK, BLOCK)
         for quad in range(4):
             queue = nc.sync if quad % 2 == 0 else nc.scalar
             queue.dma_start(out_scales[4 * quad : 4 * quad + 4, :], y_scales[32 * quad : 32 * quad + 4, :].bitcast(I32))

@@ -46,7 +46,7 @@ def tile_picked_wkv8_none_po_kernel(tc, x_words, x_scales, w1, w2, w3, num, den,
             return raw
 
         def load_plane(table, name, t):
-            plane = keep.tile([P, S], F32, name="%s%d" % (name, t))
+            plane = keep.tile([P, S], F32, name="%s%d" % (name, t), tag="%s%d" % (name, t))
             nc.sync.dma_start(plane[:], table.rearrange("(p t) s -> p t s", t=PACK)[:, t, :])
             return plane
 
@@ -114,31 +114,33 @@ def tile_picked_wkv8_none_po_kernel(tc, x_words, x_scales, w1, w2, w3, num, den,
                 nc.scalar.activation(out=made[:, :, t, :], in_=product(weight, t, first_bank + t), func=func, scale=0.5)
             return made
 
-        q1 = quantize_weight(round_weight(raw1, "w1", 64, "w1_bf"), "w1")
-        ek = []
-        for t in range(PACK):
-            plane = keep.tile([P, 2, HALF], F32, name="ek%d" % t)
-            nc.scalar.activation(out=plane[:], in_=product(q1, t, t), func=ACT.Exp, scale=0.5)
-            ek.append(plane)
-        q2 = quantize_weight(round_weight(raw2, "w2", 36, "w2_bf"), "w2")
+        q1 = quantize_weight(round_weight(raw1, "w1", 58, "w1_bf"), "w1")
+        ek = {}
+        for t in (2, 3, 0, 1):
+            ek[t] = keep.tile([P, 2, HALF], F32, name="ek%d" % t)
+            nc.scalar.activation(out=ek[t][:], in_=product(q1, t, t), func=ACT.Exp, scale=0.5)
+        q2 = quantize_weight(round_weight(raw2, "w2", 30, "w2_bf"), "w2")
 
-        dsum = halves("dsum")
-        for t in range(2):
-            nc.vector.tensor_tensor(dsum[:, :, t, :], den_early[:, t, :].rearrange("p (h s) -> p h s", h=2), ek[t][:], ALU.add)
+        dsum_high = keep.tile([P, 2, 2, HALF], F32, name="dsum_high")
         for t in range(2, PACK):
             for h in range(2):
-                nc.vector.tensor_tensor(dsum[:, h, t, :], picked(den_sb[t], h), ek[t][:, h, :], ALU.add)
+                nc.vector.tensor_tensor(dsum_high[:, h, t - 2, :], picked(den_sb[t], h), ek[t][:, h, :], ALU.add)
+        dsum_low = keep.tile([P, 2, 2, HALF], F32, name="dsum_low", tag="den3")
+        for t in range(2):
+            nc.gpsimd.tensor_tensor(dsum_low[:, :, t, :], den_early[:, t, :].rearrange("p (h s) -> p h s", h=2), ek[t][:], ALU.add)
+        dsum = (dsum_low, dsum_high)
+
+        share = halves("share")
+        for t in range(PACK):
+            nc.vector.tensor_tensor(share[:, :, t, :], product(q2, t, PACK + t), ek[t][:], ALU.mult)
 
         q3 = quantize_weight(round_weight(raw3, "w3", P, "w1_codes"), "w3")
         sign = halves("sign", "w3_raw")
-        for h in range(2):
-            nc.scalar.activation(out=sign[:, h], in_=dsum[:, h], func=ACT.Sign)
+        for pair in (1, 0):
+            nc.scalar.activation(out=sign[:, :, 2 * pair : 2 * pair + 2, :], in_=dsum[pair][:], func=ACT.Sign)
         th = activate(q3, "th", ACT.Tanh, 0)
 
-        share = halves("share", "w1_codes", 64)
-        for t in range(PACK):
-            nc.vector.tensor_tensor(share[:, :, t, :], product(q2, t, PACK + t), ek[t][:], ALU.mult)
-        nsum = halves("nsum")
+        nsum = halves("nsum", "w1_codes", 64)
         for h in range(2):
             for t in range(PACK):
                 nc.vector.tensor_tensor(nsum[:, h, t, :], picked(num_sb[t], h), share[:, h, t, :], ALU.add)
@@ -146,7 +148,8 @@ def tile_picked_wkv8_none_po_kernel(tc, x_words, x_scales, w1, w2, w3, num, den,
         inv = halves("inv")
         for h in range(2):
             root = keep.tile([P, PACK, HALF], F32, name="root", tag="w3_codes", align_bytes=64)
-            nc.scalar.activation(out=root[:], in_=dsum[:, h], func=ACT.Abs_reciprocal_sqrt)
+            for pair in range(2):
+                nc.scalar.activation(out=root[:, 2 * pair : 2 * pair + 2, :], in_=dsum[pair][:, h], func=ACT.Abs_reciprocal_sqrt)
             nc.scalar.activation(out=inv[:, h], in_=root[:], func=ACT.Square)
 
         out_rows = out_0.rearrange("(p t) s -> p t s", t=PACK)
@@ -157,7 +160,7 @@ def tile_picked_wkv8_none_po_kernel(tc, x_words, x_scales, w1, w2, w3, num, den,
 
         def make_y(h, factor_tag):
             factor = keep.tile([P, 2, PACK, BLOCK], F32, name="factor", tag=factor_tag, align_bytes=64)
-            gate = keep.tile([P, 2, PACK, BLOCK], F32, name="gate", tag="gate")
+            gate = keep.tile([P, 2, PACK, BLOCK], F32, name="gate", tag="gate%d" % h)
             for b in range(2):
                 nc.vector.scalar_tensor_tensor(gate[:, b], block(th, 2 * h + b), 1.0, block(sign, 2 * h + b), ALU.add, ALU.mult)
             for b in range(2):

from contextlib import ExitStack

import concourse.mybir as mybir

K, T, S, N = 512, 2048, 512, 512
FLOPS = 3 * 2 * K * N * S

F32 = mybir.dt.float32
BF16 = mybir.dt.bfloat16
I32 = mybir.dt.int32
U32 = mybir.dt.uint32
U16 = mybir.dt.uint16
U8 = mybir.dt.uint8
FP8X4 = mybir.dt.float8_e4m3fn_x4
ACT = mybir.ActivationFunctionType
ALU = mybir.AluOpType

P = 128
PACK = 4
HALF = S // 2
LIST_COLS = HALF // 16
BLOCK = 128


def tile_picked_wkv8_none_po_kernel(tc, x_words, x_scales, w1, w2, w3, num, den, offs, par, out_0, out_1, out_2):
    nc = tc.nc
    with ExitStack() as ctx:
        lists = ctx.enter_context(tc.tile_pool(name="lists", bufs=1))
        keep = ctx.enter_context(tc.tile_pool(name="keep", bufs=1))
        psum = ctx.enter_context(tc.psum_pool(name="psum", bufs=1))

        offs_sb = lists.tile([P, S // 16], U16, name="offs_sb")
        par_sb = lists.tile([P, S // 16], U16, name="par_sb")
        warm = keep.tile([P, 8], F32, name="warm")
        warm_out = keep.tile([P, 8], F32, name="warm_out")
        nc.vector.memset(warm[:], 0.0)
        nc.scalar.activation(out=warm_out[:], in_=warm[:], func=ACT.Exp)

        xw = keep.tile([P, T], I32, name="xw")
        xs = keep.tile([P, T], U8, name="xs")
        nc.gpsimd.memset(xs[:].bitcast(I32), 0)

        def load_weight(w, name):
            raw = keep.tile([P, PACK, N], F32, name=name + "_raw", tag=name + "_raw")
            nc.sync.dma_start(raw[:], w.rearrange("(p j) n -> p j n", j=PACK))
            return raw

        def load_plane(table, name, t):
            plane = keep.tile([P, S], F32, name="%s%d" % (name, t), tag="%s%d" % (name, t))
            nc.sync.dma_start(plane[:], table.rearrange("(p t) s -> p t s", t=PACK)[:, t, :])
            return plane

        den_sb = []
        nc.sync.dma_start(par_sb[:], par)
        den_sb.append(load_plane(den, "den", 0))
        den_sb.append(load_plane(den, "den", 1))
        for quad in range(4):
            nc.sync.dma_start(xs[32 * quad : 32 * quad + 4, :].bitcast(I32), x_scales[0, 4 * quad : 4 * quad + 4, :].bitcast(I32))
        nc.sync.dma_start(xw[:], x_words[0].rearrange("p n r -> p (n r)").bitcast(I32))
        nc.sync.dma_start(offs_sb[:], offs)
        raw1 = load_weight(w1, "w1")
        raw2 = load_weight(w2, "w2")
        den_sb.append(load_plane(den, "den", 2))
        den_sb.append(load_plane(den, "den", 3))
        raw3 = load_weight(w3, "w3")
        num_sb = [load_plane(num, "num", t) for t in range(PACK)]

        def halves(name, tag=None, align_bytes=None):
            return keep.tile([P, 2, PACK, HALF], F32, name=name, tag=tag or name, align_bytes=align_bytes)

        def block(tile, u):
            return tile[:, u // 2, :, u % 2 * BLOCK : (u % 2 + 1) * BLOCK]

        def picked(plane, h):
            return plane[:].indirect(par_sb[:, h * LIST_COLS : (h + 1) * LIST_COLS])

        def round_weight(raw, name, split, tag):
            dealt = keep.tile([P, PACK, P, PACK], BF16, name=name + "_bf", tag=tag, align_bytes=64)
            src = raw[:].rearrange("p j (m t) -> p m t j", t=PACK)
            dst = dealt[:].rearrange("p t m j -> p m t j")
            if split > 0:
                nc.scalar.copy(dst[:, :split], src[:, :split])
            if split < P:
                nc.vector.tensor_copy(dst[:, split:], src[:, split:])
            return dealt

        def quantize_weight(dealt, name):
            codes = keep.tile([P, N], U32, name=name + "_codes", tag=name + "_codes", align_bytes=64)
            scales = keep.tile([P, N], U8, name=name + "_scales", align_bytes=64)
            nc.vector.quantize_mx(out=codes[:].bitcast(FP8X4), scales=scales[:], in_=dealt[:].rearrange("p t m j -> p (t m j)"))
            return codes, scales

        den_early = keep.tile([P, 2, S], F32, name="den_early")
        for t in range(2):
            for h in range(2):
                nc.vector.tensor_copy(den_early[:, t, h * HALF : (h + 1) * HALF], picked(den_sb[t], h))

        xg_words = keep.tile([P, S], U32, name="xg_words", align_bytes=64)
        xg_scales = keep.tile([P, S], U8, name="xg_scales", align_bytes=64)
        nc.vector.tensor_copy(xg_words[:], xw[:].bitcast(U32).indirect(offs_sb[:]))
        nc.vector.tensor_copy(xg_scales[:], xs[:].indirect(offs_sb[:]))

        def product(weight, t, bank):
            codes, scales = weight
            acc = psum.tile([P, S], F32, name="bank%d" % bank, tag="bank%d" % bank)
            cols = slice(t * P, (t + 1) * P)
            nc.tensor.matmul_mx(out=acc[:], lhsT=codes[:, cols].bitcast(FP8X4), lhsT_scale=scales[:, cols],
                                rhs=xg_words[:].bitcast(FP8X4), rhs_scale=xg_scales[:], start=True, stop=True)
            return acc[:].rearrange("p (h s) -> p h s", h=2)

        def activate(weight, name, func, first_bank):
            made = halves(name)
            for t in range(PACK):
                nc.scalar.activation(out=made[:, :, t, :], in_=product(weight, t, first_bank + t), func=func, scale=0.5)
            return made

        q1 = quantize_weight(round_weight(raw1, "w1", 58, "w1_bf"), "w1")
        ek = {}
        for t in (2, 3, 0, 1):
            ek[t] = keep.tile([P, 2, HALF], F32, name="ek%d" % t)
            nc.scalar.activation(out=ek[t][:], in_=product(q1, t, t), func=ACT.Exp, scale=0.5)
        q2 = quantize_weight(round_weight(raw2, "w2", 30, "w2_bf"), "w2")

        dsum_high = keep.tile([P, 2, 2, HALF], F32, name="dsum_high")
        for t in range(2, PACK):
            for h in range(2):
                nc.vector.tensor_tensor(dsum_high[:, h, t - 2, :], picked(den_sb[t], h), ek[t][:, h, :], ALU.add)
        dsum_low = keep.tile([P, 2, 2, HALF], F32, name="dsum_low", tag="den3")
        for t in range(2):
            nc.gpsimd.tensor_tensor(dsum_low[:, :, t, :], den_early[:, t, :].rearrange("p (h s) -> p h s", h=2), ek[t][:], ALU.add)
        dsum = (dsum_low, dsum_high)

        share = halves("share")
        for t in range(PACK):
            nc.vector.tensor_tensor(share[:, :, t, :], product(q2, t, PACK + t), ek[t][:], ALU.mult)

        q3 = quantize_weight(round_weight(raw3, "w3", P, "w1_codes"), "w3")
        sign = halves("sign", "w3_raw")
        for pair in (1, 0):
            nc.scalar.activation(out=sign[:, :, 2 * pair : 2 * pair + 2, :], in_=dsum[pair][:], func=ACT.Sign)
        th = activate(q3, "th", ACT.Tanh, 0)

        nsum = halves("nsum", "w1_codes", 64)
        for h in range(2):
            for t in range(PACK):
                nc.vector.tensor_tensor(nsum[:, h, t, :], picked(num_sb[t], h), share[:, h, t, :], ALU.add)

        inv = halves("inv")
        for h in range(2):
            root = keep.tile([P, PACK, HALF], F32, name="root", tag="w3_codes", align_bytes=64)
            for pair in range(2):
                nc.scalar.activation(out=root[:, 2 * pair : 2 * pair + 2, :], in_=dsum[pair][:, h], func=ACT.Abs_reciprocal_sqrt)
            nc.scalar.activation(out=inv[:, h], in_=root[:], func=ACT.Square)

        out_rows = out_0.rearrange("(p t) s -> p t s", t=PACK)
        out_words = out_1[0].rearrange("p n r -> p (n r)").bitcast(I32)
        out_scales = out_2[0].bitcast(I32)
        y_scales = keep.tile([P, S], U8, name="y_scales", align_bytes=64)
        y = halves("y")

        def make_y(h, factor_tag):
            factor = keep.tile([P, 2, PACK, BLOCK], F32, name="factor", tag=factor_tag, align_bytes=64)
            gate = keep.tile([P, 2, PACK, BLOCK], F32, name="gate", tag="gate%d" % h)
            for b in range(2):
                nc.vector.scalar_tensor_tensor(gate[:, b], block(th, 2 * h + b), 1.0, block(sign, 2 * h + b), ALU.add, ALU.mult)
            for b in range(2):
                nc.vector.scalar_tensor_tensor(factor[:, b], gate[:, b], 0.5, block(inv, 2 * h + b), ALU.mult, ALU.mult)
            for b in range(2):
                nc.vector.tensor_tensor(block(y, 2 * h + b), block(nsum, 2 * h + b), factor[:, b], ALU.mult)

        def hand_out(first, width, copy):
            part = y[:, first // HALF, :, first % HALF : first % HALF + width]
            nc.sync.dma_start(out_rows[:, :, first : first + width], part)
            y_bf = keep.tile([P, width, PACK], BF16, name="ybf%d" % first, tag="ybf%d" % first, align_bytes=64)
            copy(y_bf[:].rearrange("p (c i) t -> p c t i", i=4), part.rearrange("p t (c i) -> p c t i", i=4))
            return y_bf

        def make_planes(y_bf, first, width):
            cols = slice(first, first + width)
            y_codes = keep.tile([P, width], I32, name="ycodes%d" % first, align_bytes=64)
            nc.vector.quantize_mx(out=y_codes[:].bitcast(FP8X4), scales=y_scales[:, cols], in_=y_bf[:].rearrange("p c t -> p (c t)"))
            nc.sync.dma_start(out_words[:, cols], y_codes[:])

        make_y(0, "factor")
        b0 = hand_out(0, HALF, nc.scalar.copy)
        make_planes(b0, 0, HALF)
        make_y(1, "factor1")
        b1 = hand_out(HALF, BLOCK, nc.scalar.copy)
        b2 = hand_out(HALF + BLOCK, BLOCK, nc.vector.tensor_copy)
        make_planes(b1, HALF, BLOCK)
        make_planes(b2, HALF + BLOCK, BLOCK)
        for quad in range(4):
            queue = nc.sync if quad % 2 == 0 else nc.scalar
            queue.dma_start(out_scales[4 * quad : 4 * quad + 4, :], y_scales[32 * quad : 32 * quad + 4, :].bitcast(I32))
